import numpy as np, ml_dtypes
CORES = [32,160,288,416,80,208,336,464]
N = 8
DEG, TK, TIMES = 3, 128, 2
MASK = [[4,6,0],[4,6,1],[4,6,2],[4,6,3],[4,6,0],[4,6,5],[4,6,0],[4,6,7]]
def setup_inputs(rng):
    return {"x": rng.standard_normal((N, 128, TK), dtype=np.float32).astype(ml_dtypes.bfloat16), "w": (rng.standard_normal((N, 128, DEG * 128), dtype=np.float32) / np.float32(np.sqrt(128 * DEG / 2))).astype(ml_dtypes.bfloat16)}
def setup_inputs_big(rng):
    d = setup_inputs(rng)
    for k in ("x",): d[k] = (d[k].astype(np.float32) * 1048576.0).astype(d[k].dtype)
    return d
def setup_inputs_small(rng):
    d = setup_inputs(rng)
    for k in ("x",): d[k] = (d[k].astype(np.float32) * (1 / 1048576.0)).astype(d[k].dtype)
    return d
def setup_inputs_apart(rng):
    d = setup_inputs(rng)
    f = (10.0 ** rng.permutation(np.linspace(-1.5, 1.5, N))).astype(np.float32).reshape(N, 1, 1)
    for k in ("x",): d[k] = (d[k].astype(np.float32) * f).astype(d[k].dtype)
    return d
def reference(x, w):
    X, W = x.astype(np.float64), w.astype(np.float64)
    h = list(X)
    for _ in range(TIMES):
        h = [np.maximum(sum(W[r][:, 128 * i:128 * i + 128].T @ h[j] for i, j in enumerate(MASK[r])), 0.0) for r in range(N)]
    return {"y": np.stack(h).astype(ml_dtypes.bfloat16)}

@@ -1,0 +1,166 @@
+from concourse.bass import DstId, RemoteDMATransfer
+from concourse.mybir import AluOpType
+
+K = 128
+SCRATCH = {
+    "own": ("sbuf", [128, 4 * K], "bfloat16"),
+    "ctr": ("sbuf", [128, 8 * K], "bfloat16"),
+    "le": ("sbuf", [128, 4 * K], "bfloat16"),
+    "hh": ("sbuf", [128, 3 * K], "bfloat16"),
+    "hown": ("sbuf", [128, K], "bfloat16"),
+    "hes": ("sbuf", [128, K], "bfloat16"),
+    "yo": ("sbuf", [128, K], "bfloat16"),
+    "zero": ("sbuf", [128, K], "float32"),
+    "p1": ("psum", [128, 512], "float32"),
+    "p2": ("psum", [128, 512], "float32"),
+    "p3": ("psum", [128, 512], "float32"),
+    "p4": ("psum", [128, 512], "float32"),
+    "p5": ("psum", [128, 512], "float32"),
+}
+SEMAPHORES = ["ld", "zs", "aA", "aB", "aE", "aH", "a0", "m1", "m5", "v1", "m2", "v2", "m3", "v3", "m4", "v4", "st", "ls"]
+
+
+def make_plan(T, topo):
+    M, cs = T.tables["MASK"], T.cores
+    n = len(cs)
+    A, B = M[0][0], M[0][1]
+    E = M[A][2]
+    ok = lambda a, b: topo.may_write(cs[a], cs[b])
+    rk = lambda r: topo.rack(topo.host(cs[r]))
+    cable = lambda a, b: rk(a) != rk(b) and topo.chip(cs[a]) == topo.chip(cs[b])
+    mid = [r for r in range(n) if r not in (A, B) and ok(A, r) and ok(B, r)]
+    cen = [r for r in mid if topo.chip(cs[r]) == topo.chip(cs[A])]
+    oth = [r for r in mid if r not in cen]
+    site = [r for r in oth if rk(r) == rk(E)][0]
+    ends = [r for r in range(n) if r not in mid and r not in (A, B)]
+    xa, xb = (3 * K, 4 * K), (4 * K, 5 * K)
+    calls = []
+    for hub, lo, xs, xd, sem in ((A, 0, (3 * K, 4 * K), xa, "aA"), (B, 4 * K, (0, K), xb, "aB")):
+        far = [c for c in cen if cable(hub, c)] + [c for c in cen if not cable(hub, c)]
+        calls.append(("hub", hub, [([c], "own", 0, 4 * K, "ctr", lo, lo + 4 * K, sem, 1 - i, 2) for i, c in enumerate(far)]))
+        for to in ([site], [r for r in oth if r != site] + [r for r in ends if ok(hub, r)]):
+            calls.append(("hubx", hub, [(to, "own", xs[0], xs[1], "ctr", xd[0], xd[1], sem, 0, 1)]))
+    calls.append(("e1", E, [([c], "own", 0, K, "le", 0, K, "aE", i, 2) for i, c in enumerate(cen)]))
+    calls.append(("e2", E, [([site], "own", 0, 4 * K, "le", 0, 4 * K, "aE", 0, 1)]))
+    for c in cen:
+        mine = [r for r in ends if rk(r) == rk(c)]
+        for r in mine:
+            for hub, xd, sem in ((A, xa, "aA"), (B, xb, "aB")):
+                if not ok(hub, r):
+                    calls.append(("fwd", c, [([r], "ctr", xd[0], xd[1], "ctr", xd[0], xd[1], sem, 0, 1)]))
+        to = [h for h in (A, B) if cable(c, h)] + mine + [r for r in oth if topo.host(cs[r]) == topo.host(cs[c])]
+        calls.append(("hh", c, [(to, "hh", 0, 2 * K, "hh", 0, 2 * K, "aH", 0, 1)]))
+    calls.append(("he", site, [([h], "hes", 0, K, "hh", 2 * K, 3 * K, "a0", i, 2) for i, h in enumerate((A, B))]))
+    return {"A": A, "B": B, "E": E, "cen": cen, "site": site, "calls": calls}
+
+
+def rank_program(g, core, T, topo):
+    rank = T.rank_of(core)
+    if rank is None:
+        return
+    P = make_plan(T, topo)
+    cs, S = T.cores, T.sem
+    A, B = P["A"], P["B"]
+    hub, centre, site = rank in (A, B), rank in P["cen"], rank == P["site"]
+
+    def engines(src, dsts, part, parts):
+        m = topo.mask(cs[src], cs[dsts[0]])
+        for d in dsts:
+            m &= topo.mask(cs[src], cs[d])
+        sel = [b for b in range(m.bit_length()) if (m >> b) & 1][part::parts]
+        return sum(1 << b for b in sel), len(sel)
+
+    def expect(sem):
+        return sum(engines(src, t[0], t[8], t[9])[1] for _, src, trs in P["calls"] for t in trs if t[7] == sem and rank in t[0])
+
+    sent = [0]
+
+    def issue(key):
+        for k, src, trs in P["calls"]:
+            if k != key or src != rank:
+                continue
+            lst = []
+            for to, sb, s0, s1, db, d0, d1, sem, part, parts in trs:
+                m, ne = engines(src, to, part, parts)
+                ids = [DstId(rid=a[0], pnc=a[1]) for a in (topo.addr(cs[d], core) for d in to)]
+                lst.append(RemoteDMATransfer(dst_ids=ids, dma_engine_mask=m, remote_sem=S[sem], srcs=[T[sb][:, s0:s1]],
+                                             dsts=[T[db][:, d0:d1] for _ in to], alu_op=0))
+                sent[0] += ne
+            g.remote_dma_fused(lst, local_sem=S.ls)
+
+    te, ve = g.tensor, g.vector
+    xo = 3 * K if rank == A else 0
+    wo = 0 if rank == A else K
+    x_own = T.own[:, xo:xo + K]
+    W = [T.own[:, wo + i * K:wo + (i + 1) * K] for i in range(3)]
+    x_a, x_b = T.ctr[:, 3 * K:4 * K], T.ctr[:, 4 * K:5 * K]
+    cnt = {}
+
+    def mm(ps, sem, terms, first=True, last=True):
+        for i, (l, r) in enumerate(terms):
+            te.matmul(ps, l, r, start=first and i == 0, stop=last and i == len(terms) - 1).then_inc(S[sem], 1)
+            cnt[sem] = cnt.get(sem, 0) + 1
+
+    def relu(out, ps, msem, vsem):
+        ve.wait_ge(S[msem], cnt[msem])
+        ve.tensor_tensor(out, ps, T.zero[:], AluOpType.max).then_inc(S[vsem], 1)
+
+    g.sync.dma_start(x_own, T.x[:]).then_inc(S.ld, 16)
+    g.scalar.dma_start(T.own[:, wo:wo + 3 * K], T.w[:]).then_inc(S.ld, 16)
+    ve.memset(T.zero[:], 0.0).then_inc(S.zs, 1)
+    ve.wait_ge(S.zs, 1)
+
+    if hub or rank == P["E"]:
+        g.wait_ge(S.ld, 32)
+        issue("hub"); issue("hubx"); issue("e1"); issue("e2")
+    if centre:
+        g.wait_ge(S.aA, expect("aA")); g.wait_ge(S.aB, expect("aB"))
+        issue("fwd")
+        g.wait_ge(S.v1, 2)
+        issue("hh")
+    if site:
+        g.wait_ge(S.v4, 1)
+        issue("he")
+
+    if centre:
+        WA = [T.ctr[:, i * K:(i + 1) * K] for i in range(3)]
+        WB = [T.ctr[:, (5 + i) * K:(6 + i) * K] for i in range(3)]
+        x_e = T.le[:, 0:K]
+        te.wait_ge(S.aE, expect("aE")); te.wait_ge(S.aA, expect("aA"))
+        mm(T.p1[:, 0:K], "m1", [(WA[0], x_a), (WA[2], x_e)], last=False)
+        te.wait_ge(S.aB, expect("aB"))
+        mm(T.p1[:, 0:K], "m1", [(WA[1], x_b)], first=False)
+        mm(T.p5[:, 0:K], "m5", [(WB[0], x_a), (WB[1], x_b), (WB[2], x_e)])
+        relu(T.hh[:, 0:K], T.p1[:, 0:K], "m1", "v1")
+        relu(T.hh[:, K:2 * K], T.p5[:, 0:K], "m5", "v1")
+    if site:
+        te.wait_ge(S.aE, expect("aE")); te.wait_ge(S.aA, expect("aA")); te.wait_ge(S.aB, expect("aB"))
+        mm(T.p4[:, 0:K], "m4", [(T.le[:, 3 * K:4 * K], T.le[:, 0:K]), (T.le[:, K:2 * K], x_a), (T.le[:, 2 * K:3 * K], x_b)])
+        relu(T.hes[:], T.p4[:, 0:K], "m4", "v4")
+    te.wait_ge(S.ld, 32)
+    if hub:
+        te.wait_ge(S.aH, expect("aH"))
+        mm(T.p3[:, 0:K], "m3", [(W[0], T.hh[:, 0:K]), (W[1], T.hh[:, K:2 * K])], last=False)
+        te.wait_ge(S.a0, expect("a0"))
+        mm(T.p3[:, 0:K], "m3", [(W[2], T.hh[:, 2 * K:3 * K])], first=False)
+    else:
+        mm(T.p2[:, 0:K], "m2", [(W[2], x_own)], last=False)
+        te.wait_ge(S.aA, expect("aA"))
+        mm(T.p2[:, 0:K], "m2", [(W[0], x_a)], first=False, last=False)
+        te.wait_ge(S.aB, expect("aB"))
+        mm(T.p2[:, 0:K], "m2", [(W[1], x_b)], first=False)
+        relu(T.hown[:], T.p2[:, 0:K], "m2", "v2")
+        te.wait_ge(S.v2, 1)
+        mm(T.p3[:, 0:K], "m3", [(W[2], T.hown[:])], last=False)
+        if centre:
+            te.wait_ge(S.v1, 2)
+        else:
+            te.wait_ge(S.aH, expect("aH"))
+        mm(T.p3[:, 0:K], "m3", [(W[0], T.hh[:, 0:K]), (W[1], T.hh[:, K:2 * K])], first=False)
+    relu(T.yo[:], T.p3[:, 0:K], "m3", "v3")
+
+    g.sync.wait_ge(S.v3, 1)
+    g.sync.dma_start(T.y[:], T.yo[:]).then_inc(S.st, 16)
+    if sent[0]:
+        g.wait_ge(S.ls, sent[0])
+    g.wait_ge(S.st, 16)

@@ -17,7 +17,7 @@ SCRATCH = {
     "p4": ("psum", [128, 512], "float32"),
     "p5": ("psum", [128, 512], "float32"),
 }
-SEMAPHORES = ["ld", "zs", "aA", "aB", "aE", "aH", "a0", "m1", "m5", "v1", "m2", "v2", "m3", "v3", "m4", "v4", "st", "ls"]
+SEMAPHORES = ["lx", "ld", "zs", "aX", "aA", "aB", "aE", "aH", "a0", "m1", "m5", "v1", "m2", "v2", "m3", "v3", "m4", "v4", "st", "ls"]
 
 
 def make_plan(T, topo):
@@ -34,12 +34,18 @@ def make_plan(T, topo):
     site = [r for r in oth if rk(r) == rk(E)][0]
     ends = [r for r in range(n) if r not in mid and r not in (A, B)]
     xa, xb = (3 * K, 4 * K), (4 * K, 5 * K)
+    cabhub = {c: [h for h in (A, B) if cable(h, c)][0] for c in cen}
+    sitecen = [c for c in cen if topo.host(cs[c]) == topo.host(cs[site])][0]
     calls = []
     for hub, lo, xs, xd, sem in ((A, 0, (3 * K, 4 * K), xa, "aA"), (B, 4 * K, (0, K), xb, "aB")):
-        far = [c for c in cen if cable(hub, c)] + [c for c in cen if not cable(hub, c)]
-        calls.append(("hub", hub, [([c], "own", 0, 4 * K, "ctr", lo, lo + 4 * K, sem, 1 - i, 2) for i, c in enumerate(far)]))
-        for to in ([site], [r for r in oth if r != site] + [r for r in ends if ok(hub, r)]):
-            calls.append(("hubx", hub, [(to, "own", xs[0], xs[1], "ctr", xd[0], xd[1], sem, 0, 1)]))
+        cab, sw = [c for c in cen if cable(hub, c)] + [c for c in cen if not cable(hub, c)]
+        w0 = 0 if xs[0] else K
+        calls.append(("hx0", hub, [([cab], "own", xs[0], xs[1], "ctr", xd[0], xd[1], "aX", 1, 2)]))
+        calls.append(("hub", hub, [([sw], "own", 0, 4 * K, "ctr", lo, lo + 4 * K, sem, 0, 2)]))
+        calls.append(("hub", hub, [([cab], "own", w0, w0 + 3 * K, "ctr", lo + w0, lo + w0 + 3 * K, sem, 1, 2)]))
+        for to in ([site] if cabhub[sitecen] != hub else [], [r for r in oth if r != site] + [r for r in ends if ok(hub, r)]):
+            if to:
+                calls.append(("hubx", hub, [(to, "own", xs[0], xs[1], "ctr", xd[0], xd[1], sem, 0, 1)]))
     calls.append(("e1", E, [([c], "own", 0, K, "le", 0, K, "aE", i, 2) for i, c in enumerate(cen)]))
     calls.append(("e2", E, [([site], "own", 0, 4 * K, "le", 0, 4 * K, "aE", 0, 1)]))
     for c in cen:
@@ -47,11 +53,15 @@ def make_plan(T, topo):
         for r in mine:
             for hub, xd, sem in ((A, xa, "aA"), (B, xb, "aB")):
                 if not ok(hub, r):
-                    calls.append(("fwd", c, [([r], "ctr", xd[0], xd[1], "ctr", xd[0], xd[1], sem, 0, 1)]))
-        to = [h for h in (A, B) if cable(c, h)] + mine + [r for r in oth if topo.host(cs[r]) == topo.host(cs[c])]
+                    if c == sitecen:
+                        calls.append(("fwd", c, [([site], "ctr", xd[0], xd[1], "ctr", xd[0], xd[1], sem, 0, 1)]))
+                        calls.append(("fw2", site, [([r], "ctr", xd[0], xd[1], "ctr", xd[0], xd[1], sem, 0, 1)]))
+                    else:
+                        calls.append(("fwd", c, [([r], "ctr", xd[0], xd[1], "ctr", xd[0], xd[1], sem, 0, 1)]))
+        to = [cabhub[c]] + [r for r in oth if topo.host(cs[r]) == topo.host(cs[c])] + mine
         calls.append(("hh", c, [(to, "hh", 0, 2 * K, "hh", 0, 2 * K, "aH", 0, 1)]))
     calls.append(("he", site, [([h], "hes", 0, K, "hh", 2 * K, 3 * K, "a0", i, 2) for i, h in enumerate((A, B))]))
-    return {"A": A, "B": B, "E": E, "cen": cen, "site": site, "calls": calls}
+    return {"A": A, "B": B, "E": E, "cen": cen, "site": site, "calls": calls, "cabhub": cabhub, "early": cabhub[sitecen]}
 
 
 def rank_program(g, core, T, topo):
@@ -62,6 +72,7 @@ def rank_program(g, core, T, topo):
     cs, S = T.cores, T.sem
     A, B = P["A"], P["B"]
     hub, centre, site = rank in (A, B), rank in P["cen"], rank == P["site"]
+    hsem = {A: "aA", B: "aB"}
 
     def engines(src, dsts, part, parts):
         m = topo.mask(cs[src], cs[dsts[0]])
@@ -105,39 +116,51 @@ def rank_program(g, core, T, topo):
         ve.wait_ge(S[msem], cnt[msem])
         ve.tensor_tensor(out, ps, T.zero[:], AluOpType.max).then_inc(S[vsem], 1)
 
-    g.sync.dma_start(x_own, T.x[:]).then_inc(S.ld, 16)
+    g.sync.dma_start(x_own, T.x[:]).then_inc(S.lx, 16)
     g.scalar.dma_start(T.own[:, wo:wo + 3 * K], T.w[:]).then_inc(S.ld, 16)
     ve.memset(T.zero[:], 0.0).then_inc(S.zs, 1)
     ve.wait_ge(S.zs, 1)
 
     if hub or rank == P["E"]:
-        g.wait_ge(S.ld, 32)
-        issue("hub"); issue("hubx"); issue("e1"); issue("e2")
+        g.wait_ge(S.lx, 16)
+        issue("hx0"); issue("e1")
+        g.wait_ge(S.ld, 16)
+        issue("hub"); issue("hubx"); issue("e2")
     if centre:
-        g.wait_ge(S.aA, expect("aA")); g.wait_ge(S.aB, expect("aB"))
+        g.wait_ge(S.aX, expect("aX"))
         issue("fwd")
         g.wait_ge(S.v1, 2)
         issue("hh")
     if site:
+        g.wait_ge(S[hsem[P["early"]]], expect(hsem[P["early"]]))
+        issue("fw2")
         g.wait_ge(S.v4, 1)
         issue("he")
 
     if centre:
-        WA = [T.ctr[:, i * K:(i + 1) * K] for i in range(3)]
-        WB = [T.ctr[:, (5 + i) * K:(6 + i) * K] for i in range(3)]
         x_e = T.le[:, 0:K]
-        te.wait_ge(S.aE, expect("aE")); te.wait_ge(S.aA, expect("aA"))
-        mm(T.p1[:, 0:K], "m1", [(WA[0], x_a), (WA[2], x_e)], last=False)
-        te.wait_ge(S.aB, expect("aB"))
-        mm(T.p1[:, 0:K], "m1", [(WA[1], x_b)], first=False)
-        mm(T.p5[:, 0:K], "m5", [(WB[0], x_a), (WB[1], x_b), (WB[2], x_e)])
-        relu(T.hh[:, 0:K], T.p1[:, 0:K], "m1", "v1")
-        relu(T.hh[:, K:2 * K], T.p5[:, 0:K], "m5", "v1")
+        tiles = {A: [T.ctr[:, i * K:(i + 1) * K] for i in range(3)], B: [T.ctr[:, (5 + i) * K:(6 + i) * K] for i in range(3)]}
+        out = {A: T.hh[:, 0:K], B: T.hh[:, K:2 * K]}
+        late = P["cabhub"][rank]
+        soon = B if late == A else A
+        te.wait_ge(S.aX, expect("aX")); te.wait_ge(S.aE, expect("aE")); te.wait_ge(S[hsem[soon]], expect(hsem[soon]))
+        mm(T.p1[:, 0:K], "m1", [(tiles[soon][0], x_a), (tiles[soon][1], x_b), (tiles[soon][2], x_e)])
+        te.wait_ge(S[hsem[late]], expect(hsem[late]))
+        mm(T.p5[:, 0:K], "m5", [(tiles[late][0], x_a), (tiles[late][1], x_b), (tiles[late][2], x_e)])
+        relu(out[soon], T.p1[:, 0:K], "m1", "v1")
+        relu(out[late], T.p5[:, 0:K], "m5", "v1")
     if site:
-        te.wait_ge(S.aE, expect("aE")); te.wait_ge(S.aA, expect("aA")); te.wait_ge(S.aB, expect("aB"))
-        mm(T.p4[:, 0:K], "m4", [(T.le[:, 3 * K:4 * K], T.le[:, 0:K]), (T.le[:, K:2 * K], x_a), (T.le[:, 2 * K:3 * K], x_b)])
+        xs = {A: (T.le[:, K:2 * K], x_a), B: (T.le[:, 2 * K:3 * K], x_b)}
+        h0 = P["early"]
+        h1 = B if h0 == A else A
+        te.wait_ge(S.aE, expect("aE"))
+        mm(T.p4[:, 0:K], "m4", [(T.le[:, 3 * K:4 * K], T.le[:, 0:K])], last=False)
+        te.wait_ge(S[hsem[h0]], expect(hsem[h0]))
+        mm(T.p4[:, 0:K], "m4", [xs[h0]], first=False, last=False)
+        te.wait_ge(S[hsem[h1]], expect(hsem[h1]))
+        mm(T.p4[:, 0:K], "m4", [xs[h1]], first=False)
         relu(T.hes[:], T.p4[:, 0:K], "m4", "v4")
-    te.wait_ge(S.ld, 32)
+    te.wait_ge(S.lx, 16); te.wait_ge(S.ld, 16)
     if hub:
         te.wait_ge(S.aH, expect("aH"))
         mm(T.p3[:, 0:K], "m3", [(W[0], T.hh[:, 0:K]), (W[1], T.hh[:, K:2 * K])], last=False)

@@ -17,7 +17,8 @@ SCRATCH = {
     "p4": ("psum", [128, 512], "float32"),
     "p5": ("psum", [128, 512], "float32"),
 }
-SEMAPHORES = ["lx", "ld", "zs", "aX", "aA", "aB", "aE", "aH", "a0", "m1", "m5", "v1", "m2", "v2", "m3", "v3", "m4", "v4", "st", "ls"]
+SEMAPHORES = ["lx", "ld", "zs", "aX", "aA", "aB", "aE", "aH", "a0", "m1", "m5", "v1", "v5", "m2", "v2", "m3", "v3", "m4", "v4",
+              "st", "ls"]
 
 
 def make_plan(T, topo):
@@ -47,21 +48,28 @@ def make_plan(T, topo):
             if to:
                 calls.append(("hubx", hub, [(to, "own", xs[0], xs[1], "ctr", xd[0], xd[1], sem, 0, 1)]))
     calls.append(("e1", E, [([c], "own", 0, K, "le", 0, K, "aE", i, 2) for i, c in enumerate(cen)]))
+    relay = [r for r in oth if r != site][0]
+    calls.append(("e3", E, [([relay] + [h for h in (A, B) if ok(E, h)], "own", 0, K, "le", 0, K, "aE", 0, 1)]))
+    calls.append(("fe", relay, [([h for h in (A, B) if not ok(E, h)], "le", 0, K, "le", 0, K, "aE", 0, 1)]))
     calls.append(("e2", E, [([site], "own", 0, 4 * K, "le", 0, 4 * K, "aE", 0, 1)]))
     for c in cen:
         mine = [r for r in ends if rk(r) == rk(c)]
         for r in mine:
             for hub, xd, sem in ((A, xa, "aA"), (B, xb, "aB")):
                 if not ok(hub, r):
+                    near = [h for h in (A, B) if h != hub]
                     if c == sitecen:
-                        calls.append(("fwd", c, [([site], "ctr", xd[0], xd[1], "ctr", xd[0], xd[1], sem, 0, 1)]))
+                        calls.append(("fwd", c, [([site] + near, "ctr", xd[0], xd[1], "ctr", xd[0], xd[1], sem, 0, 1)]))
                         calls.append(("fw2", site, [([r], "ctr", xd[0], xd[1], "ctr", xd[0], xd[1], sem, 0, 1)]))
                     else:
-                        calls.append(("fwd", c, [([r], "ctr", xd[0], xd[1], "ctr", xd[0], xd[1], sem, 0, 1)]))
-        to = [cabhub[c]] + [r for r in oth if topo.host(cs[r]) == topo.host(cs[c])] + mine
+                        calls.append(("fwd", c, [(near + [r], "ctr", xd[0], xd[1], "ctr", xd[0], xd[1], sem, 0, 1)]))
+        o = K if cabhub[c] == A else 0
+        calls.append(("h1", c, [([cabhub[c]], "hh", o, o + K, "hh", o, o + K, "aH", 0, 1)]))
+        to = [r for r in oth if topo.host(cs[r]) == topo.host(cs[c])] + mine
         calls.append(("hh", c, [(to, "hh", 0, 2 * K, "hh", 0, 2 * K, "aH", 0, 1)]))
     calls.append(("he", site, [([h], "hes", 0, K, "hh", 2 * K, 3 * K, "a0", i, 2) for i, h in enumerate((A, B))]))
-    return {"A": A, "B": B, "E": E, "cen": cen, "site": site, "calls": calls, "cabhub": cabhub, "early": cabhub[sitecen]}
+    return {"A": A, "B": B, "E": E, "cen": cen, "site": site, "calls": calls, "cabhub": cabhub, "early": cabhub[sitecen],
+            "relay": relay}
 
 
 def rank_program(g, core, T, topo):
@@ -123,14 +131,19 @@ def rank_program(g, core, T, topo):
 
     if hub or rank == P["E"]:
         g.wait_ge(S.lx, 16)
-        issue("hx0"); issue("e1")
+        issue("hx0"); issue("e1"); issue("e3")
         g.wait_ge(S.ld, 16)
         issue("hub"); issue("hubx"); issue("e2")
     if centre:
         g.wait_ge(S.aX, expect("aX"))
         issue("fwd")
-        g.wait_ge(S.v1, 2)
+        g.wait_ge(S.v1, 1)
+        issue("h1")
+        g.wait_ge(S.v5, 1)
         issue("hh")
+    if rank == P["relay"]:
+        g.wait_ge(S.aE, expect("aE"))
+        issue("fe")
     if site:
         g.wait_ge(S[hsem[P["early"]]], expect(hsem[P["early"]]))
         issue("fw2")
@@ -148,7 +161,7 @@ def rank_program(g, core, T, topo):
         te.wait_ge(S[hsem[late]], expect(hsem[late]))
         mm(T.p5[:, 0:K], "m5", [(tiles[late][0], x_a), (tiles[late][1], x_b), (tiles[late][2], x_e)])
         relu(out[soon], T.p1[:, 0:K], "m1", "v1")
-        relu(out[late], T.p5[:, 0:K], "m5", "v1")
+        relu(out[late], T.p5[:, 0:K], "m5", "v5")
     if site:
         xs = {A: (T.le[:, K:2 * K], x_a), B: (T.le[:, 2 * K:3 * K], x_b)}
         h0 = P["early"]
@@ -162,8 +175,18 @@ def rank_program(g, core, T, topo):
         relu(T.hes[:], T.p4[:, 0:K], "m4", "v4")
     te.wait_ge(S.lx, 16); te.wait_ge(S.ld, 16)
     if hub:
+        io, ix = (0, 1) if rank == A else (1, 0)
+        oh = B if rank == A else A
+        mm(T.p2[:, 0:K], "m2", [(W[io], x_own)], last=False)
+        te.wait_ge(S.aE, expect("aE"))
+        mm(T.p2[:, 0:K], "m2", [(W[2], T.le[:, 0:K])], first=False, last=False)
+        te.wait_ge(S[hsem[oh]], expect(hsem[oh]))
+        mm(T.p2[:, 0:K], "m2", [(W[ix], x_b if rank == A else x_a)], first=False)
+        relu(T.hown[:], T.p2[:, 0:K], "m2", "v2")
+        te.wait_ge(S.v2, 1)
+        mm(T.p3[:, 0:K], "m3", [(W[io], T.hown[:])], last=False)
         te.wait_ge(S.aH, expect("aH"))
-        mm(T.p3[:, 0:K], "m3", [(W[0], T.hh[:, 0:K]), (W[1], T.hh[:, K:2 * K])], last=False)
+        mm(T.p3[:, 0:K], "m3", [(W[ix], T.hh[:, ix * K:(ix + 1) * K])], first=False, last=False)
         te.wait_ge(S.a0, expect("a0"))
         mm(T.p3[:, 0:K], "m3", [(W[2], T.hh[:, 2 * K:3 * K])], first=False)
     else:
@@ -176,7 +199,7 @@ def rank_program(g, core, T, topo):
         te.wait_ge(S.v2, 1)
         mm(T.p3[:, 0:K], "m3", [(W[2], T.hown[:])], last=False)
         if centre:
-            te.wait_ge(S.v1, 2)
+            te.wait_ge(S.v1, 1); te.wait_ge(S.v5, 1)
         else:
             te.wait_ge(S.aH, expect("aH"))
         mm(T.p3[:, 0:K], "m3", [(W[0], T.hh[:, 0:K]), (W[1], T.hh[:, K:2 * K])], first=False)

from concourse.bass import DstId, RemoteDMATransfer
from concourse.mybir import AluOpType

K = 128
SCRATCH = {
    "own": ("sbuf", [128, 4 * K], "bfloat16"),
    "ctr": ("sbuf", [128, 8 * K], "bfloat16"),
    "le": ("sbuf", [128, 4 * K], "bfloat16"),
    "hh": ("sbuf", [128, 3 * K], "bfloat16"),
    "hown": ("sbuf", [128, K], "bfloat16"),
    "hes": ("sbuf", [128, K], "bfloat16"),
    "yo": ("sbuf", [128, K], "bfloat16"),
    "zero": ("sbuf", [128, K], "float32"),
    "p1": ("psum", [128, 512], "float32"),
    "p2": ("psum", [128, 512], "float32"),
    "p3": ("psum", [128, 512], "float32"),
    "p4": ("psum", [128, 512], "float32"),
    "p5": ("psum", [128, 512], "float32"),
}
SEMAPHORES = ["lx", "ld", "zs", "aX", "aA", "aB", "aE", "aH", "a0", "m1", "m5", "v1", "v5", "m2", "v2", "m3", "v3", "m4", "v4",
              "st", "ls"]


def make_plan(T, topo):
    M, cs = T.tables["MASK"], T.cores
    n = len(cs)
    A, B = M[0][0], M[0][1]
    E = M[A][2]
    ok = lambda a, b: topo.may_write(cs[a], cs[b])
    rk = lambda r: topo.rack(topo.host(cs[r]))
    cable = lambda a, b: rk(a) != rk(b) and topo.chip(cs[a]) == topo.chip(cs[b])
    mid = [r for r in range(n) if r not in (A, B) and ok(A, r) and ok(B, r)]
    cen = [r for r in mid if topo.chip(cs[r]) == topo.chip(cs[A])]
    oth = [r for r in mid if r not in cen]
    site = [r for r in oth if rk(r) == rk(E)][0]
    ends = [r for r in range(n) if r not in mid and r not in (A, B)]
    xa, xb = (3 * K, 4 * K), (4 * K, 5 * K)
    cabhub = {c: [h for h in (A, B) if cable(h, c)][0] for c in cen}
    sitecen = [c for c in cen if topo.host(cs[c]) == topo.host(cs[site])][0]
    calls = []
    for hub, lo, xs, xd, sem in ((A, 0, (3 * K, 4 * K), xa, "aA"), (B, 4 * K, (0, K), xb, "aB")):
        cab, sw = [c for c in cen if cable(hub, c)] + [c for c in cen if not cable(hub, c)]
        w0 = 0 if xs[0] else K
        calls.append(("hx0", hub, [([cab], "own", xs[0], xs[1], "ctr", xd[0], xd[1], "aX", 1, 2)]))
        calls.append(("hub", hub, [([sw], "own", 0, 4 * K, "ctr", lo, lo + 4 * K, sem, 0, 2)]))
        calls.append(("hub", hub, [([cab], "own", w0, w0 + 3 * K, "ctr", lo + w0, lo + w0 + 3 * K, sem, 1, 2)]))
        for to in ([site] if cabhub[sitecen] != hub else [], [r for r in oth if r != site] + [r for r in ends if ok(hub, r)]):
            if to:
                calls.append(("hubx", hub, [(to, "own", xs[0], xs[1], "ctr", xd[0], xd[1], sem, 0, 1)]))
    calls.append(("e1", E, [([c], "own", 0, K, "le", 0, K, "aE", i, 2) for i, c in enumerate(cen)]))
    relay = [r for r in oth if r != site][0]
    calls.append(("e3", E, [([relay] + [h for h in (A, B) if ok(E, h)], "own", 0, K, "le", 0, K, "aE", 0, 1)]))
    calls.append(("fe", relay, [([h for h in (A, B) if not ok(E, h)], "le", 0, K, "le", 0, K, "aE", 0, 1)]))
    calls.append(("e2", E, [([site], "own", 0, 4 * K, "le", 0, 4 * K, "aE", 0, 1)]))
    for c in cen:
        mine = [r for r in ends if rk(r) == rk(c)]
        for r in mine:
            for hub, xd, sem in ((A, xa, "aA"), (B, xb, "aB")):
                if not ok(hub, r):
                    near = [h for h in (A, B) if h != hub]
                    if c == sitecen:
                        calls.append(("fwd", c, [([site] + near, "ctr", xd[0], xd[1], "ctr", xd[0], xd[1], sem, 0, 1)]))
                        calls.append(("fw2", site, [([r], "ctr", xd[0], xd[1], "ctr", xd[0], xd[1], sem, 0, 1)]))
                    else:
                        calls.append(("fwd", c, [(near + [r], "ctr", xd[0], xd[1], "ctr", xd[0], xd[1], sem, 0, 1)]))
        o = K if cabhub[c] == A else 0
        calls.append(("h1", c, [([cabhub[c]], "hh", o, o + K, "hh", o, o + K, "aH", 0, 1)]))
        to = [r for r in oth if topo.host(cs[r]) == topo.host(cs[c])] + mine
        calls.append(("hh", c, [(to, "hh", 0, 2 * K, "hh", 0, 2 * K, "aH", 0, 1)]))
    calls.append(("he", site, [([h], "hes", 0, K, "hh", 2 * K, 3 * K, "a0", i, 2) for i, h in enumerate((A, B))]))
    return {"A": A, "B": B, "E": E, "cen": cen, "site": site, "calls": calls, "cabhub": cabhub, "early": cabhub[sitecen],
            "relay": relay}


def rank_program(g, core, T, topo):
    rank = T.rank_of(core)
    if rank is None:
        return
    P = make_plan(T, topo)
    cs, S = T.cores, T.sem
    A, B = P["A"], P["B"]
    hub, centre, site = rank in (A, B), rank in P["cen"], rank == P["site"]
    hsem = {A: "aA", B: "aB"}

    def engines(src, dsts, part, parts):
        m = topo.mask(cs[src], cs[dsts[0]])
        for d in dsts:
            m &= topo.mask(cs[src], cs[d])
        sel = [b for b in range(m.bit_length()) if (m >> b) & 1][part::parts]
        return sum(1 << b for b in sel), len(sel)

    def expect(sem):
        return sum(engines(src, t[0], t[8], t[9])[1] for _, src, trs in P["calls"] for t in trs if t[7] == sem and rank in t[0])

    sent = [0]

    def issue(key):
        for k, src, trs in P["calls"]:
            if k != key or src != rank:
                continue
            lst = []
            for to, sb, s0, s1, db, d0, d1, sem, part, parts in trs:
                m, ne = engines(src, to, part, parts)
                ids = [DstId(rid=a[0], pnc=a[1]) for a in (topo.addr(cs[d], core) for d in to)]
                lst.append(RemoteDMATransfer(dst_ids=ids, dma_engine_mask=m, remote_sem=S[sem], srcs=[T[sb][:, s0:s1]],
                                             dsts=[T[db][:, d0:d1] for _ in to], alu_op=0))
                sent[0] += ne
            g.remote_dma_fused(lst, local_sem=S.ls)

    te, ve = g.tensor, g.vector
    xo = 3 * K if rank == A else 0
    wo = 0 if rank == A else K
    x_own = T.own[:, xo:xo + K]
    W = [T.own[:, wo + i * K:wo + (i + 1) * K] for i in range(3)]
    x_a, x_b = T.ctr[:, 3 * K:4 * K], T.ctr[:, 4 * K:5 * K]
    cnt = {}

    def mm(ps, sem, terms, first=True, last=True):
        for i, (l, r) in enumerate(terms):
            te.matmul(ps, l, r, start=first and i == 0, stop=last and i == len(terms) - 1).then_inc(S[sem], 1)
            cnt[sem] = cnt.get(sem, 0) + 1

    def relu(out, ps, msem, vsem):
        ve.wait_ge(S[msem], cnt[msem])
        ve.tensor_tensor(out, ps, T.zero[:], AluOpType.max).then_inc(S[vsem], 1)

    g.sync.dma_start(x_own, T.x[:]).then_inc(S.lx, 16)
    g.scalar.dma_start(T.own[:, wo:wo + 3 * K], T.w[:]).then_inc(S.ld, 16)
    ve.memset(T.zero[:], 0.0).then_inc(S.zs, 1)
    ve.wait_ge(S.zs, 1)

    if hub or rank == P["E"]:
        g.wait_ge(S.lx, 16)
        issue("hx0"); issue("e1"); issue("e3")
        g.wait_ge(S.ld, 16)
        issue("hub"); issue("hubx"); issue("e2")
    if centre:
        g.wait_ge(S.aX, expect("aX"))
        issue("fwd")
        g.wait_ge(S.v1, 1)
        issue("h1")
        g.wait_ge(S.v5, 1)
        issue("hh")
    if rank == P["relay"]:
        g.wait_ge(S.aE, expect("aE"))
        issue("fe")
    if site:
        g.wait_ge(S[hsem[P["early"]]], expect(hsem[P["early"]]))
        issue("fw2")
        g.wait_ge(S.v4, 1)
        issue("he")

    if centre:
        x_e = T.le[:, 0:K]
        tiles = {A: [T.ctr[:, i * K:(i + 1) * K] for i in range(3)], B: [T.ctr[:, (5 + i) * K:(6 + i) * K] for i in range(3)]}
        out = {A: T.hh[:, 0:K], B: T.hh[:, K:2 * K]}
        late = P["cabhub"][rank]
        soon = B if late == A else A
        te.wait_ge(S.aX, expect("aX")); te.wait_ge(S.aE, expect("aE")); te.wait_ge(S[hsem[soon]], expect(hsem[soon]))
        mm(T.p1[:, 0:K], "m1", [(tiles[soon][0], x_a), (tiles[soon][1], x_b), (tiles[soon][2], x_e)])
        te.wait_ge(S[hsem[late]], expect(hsem[late]))
        mm(T.p5[:, 0:K], "m5", [(tiles[late][0], x_a), (tiles[late][1], x_b), (tiles[late][2], x_e)])
        relu(out[soon], T.p1[:, 0:K], "m1", "v1")
        relu(out[late], T.p5[:, 0:K], "m5", "v5")
    if site:
        xs = {A: (T.le[:, K:2 * K], x_a), B: (T.le[:, 2 * K:3 * K], x_b)}
        h0 = P["early"]
        h1 = B if h0 == A else A
        te.wait_ge(S.aE, expect("aE"))
        mm(T.p4[:, 0:K], "m4", [(T.le[:, 3 * K:4 * K], T.le[:, 0:K])], last=False)
        te.wait_ge(S[hsem[h0]], expect(hsem[h0]))
        mm(T.p4[:, 0:K], "m4", [xs[h0]], first=False, last=False)
        te.wait_ge(S[hsem[h1]], expect(hsem[h1]))
        mm(T.p4[:, 0:K], "m4", [xs[h1]], first=False)
        relu(T.hes[:], T.p4[:, 0:K], "m4", "v4")
    te.wait_ge(S.lx, 16); te.wait_ge(S.ld, 16)
    if hub:
        io, ix = (0, 1) if rank == A else (1, 0)
        oh = B if rank == A else A
        mm(T.p2[:, 0:K], "m2", [(W[io], x_own)], last=False)
        te.wait_ge(S.aE, expect("aE"))
        mm(T.p2[:, 0:K], "m2", [(W[2], T.le[:, 0:K])], first=False, last=False)
        te.wait_ge(S[hsem[oh]], expect(hsem[oh]))
        mm(T.p2[:, 0:K], "m2", [(W[ix], x_b if rank == A else x_a)], first=False)
        relu(T.hown[:], T.p2[:, 0:K], "m2", "v2")
        te.wait_ge(S.v2, 1)
        mm(T.p3[:, 0:K], "m3", [(W[io], T.hown[:])], last=False)
        te.wait_ge(S.aH, expect("aH"))
        mm(T.p3[:, 0:K], "m3", [(W[ix], T.hh[:, ix * K:(ix + 1) * K])], first=False, last=False)
        te.wait_ge(S.a0, expect("a0"))
        mm(T.p3[:, 0:K], "m3", [(W[2], T.hh[:, 2 * K:3 * K])], first=False)
    else:
        mm(T.p2[:, 0:K], "m2", [(W[2], x_own)], last=False)
        te.wait_ge(S.aA, expect("aA"))
        mm(T.p2[:, 0:K], "m2", [(W[0], x_a)], first=False, last=False)
        te.wait_ge(S.aB, expect("aB"))
        mm(T.p2[:, 0:K], "m2", [(W[1], x_b)], first=False)
        relu(T.hown[:], T.p2[:, 0:K], "m2", "v2")
        te.wait_ge(S.v2, 1)
        mm(T.p3[:, 0:K], "m3", [(W[2], T.hown[:])], last=False)
        if centre:
            te.wait_ge(S.v1, 1); te.wait_ge(S.v5, 1)
        else:
            te.wait_ge(S.aH, expect("aH"))
        mm(T.p3[:, 0:K], "m3", [(W[0], T.hh[:, 0:K]), (W[1], T.hh[:, K:2 * K])], first=False)
    relu(T.yo[:], T.p3[:, 0:K], "m3", "v3")

    g.sync.wait_ge(S.v3, 1)
    g.sync.dma_start(T.y[:], T.yo[:]).then_inc(S.st, 16)
    if sent[0]:
        g.wait_ge(S.ls, sent[0])
    g.wait_ge(S.st, 16)
